import numpy as np
import ml_dtypes


def mxq(x, axis, fmt="e4m3"):
    dtype, down = {"e4m3": (ml_dtypes.float8_e4m3fn, 7), "e5m2": (ml_dtypes.float8_e5m2, 14)}[fmt]
    v = np.moveaxis(np.asarray(x, np.float32).astype(ml_dtypes.bfloat16).astype(np.float64), axis, -1)
    blocks = v.reshape(v.shape[:-1] + (-1, 32))
    amax = np.abs(blocks).max(-1, keepdims=True)
    byte = np.maximum(np.where(amax > 0, np.frexp(amax)[1] - 1 + 127, 0) - down, 1)
    scale = np.exp2(byte - 127.0)
    codes = (blocks / scale).astype(np.float32).astype(dtype).astype(np.float64)
    return np.moveaxis((codes * scale).reshape(v.shape), -1, axis)


WIDE = False


def mx_kscale(k, group=512):
    if not WIDE:
        return np.ones(k)
    levels = np.array([10, -10, 5, -5, 0])
    if group != 512:
        return np.exp2(np.random.permutation(np.resize(levels, k // group))).repeat(group)
    if k % 512:
        return np.exp2(np.random.permutation(np.resize(levels, k // 32))).repeat(32)
    a = np.empty((k // 512, 16))
    for p in range(k // 512):
        a[p, :8] = np.random.permutation(np.resize(levels, 8))
        for g in range(8):
            far = levels[np.abs(levels - a[p, g]) >= 10]
            a[p, g + 8] = far[np.random.randint(len(far))]
    return np.exp2(a.ravel()).repeat(32)


def f64(x):
    return np.asarray(x).astype(np.float64)


def striped(idx):
    return np.tile(np.asarray(idx).reshape(-1, 16).T, (8, 1)).astype(np.uint16)


def unstriped(offs):
    return offs[:16].T.reshape(-1).astype(np.int64)


H, KV, D, NQ, N = 4, 4, 128, 512, 1024


def setup_inputs():
    n = np.random.standard_normal
    s = mx_kscale(D, 0)[:, None]
    u = mx_kscale(N)
    t = np.random.uniform(0.5, 2.0, N) * u
    v = n((KV, N, 128))
    v[:, :, 127] = 1.0
    return {
        "qT": (n((H, D, NQ)) * s * (0.70 / np.sqrt(D))).astype(np.float32),
        "kT": (n((KV, D, N)) / s).astype(np.float32),
        "t": t.reshape(N, 1).astype(np.float32),
        "v": (v / t[:, None]).astype(np.float32),
        "kb": (0.5 * n((N, 1))).astype(np.float32),
    }


def reference(qT, kT, t, v, kb):
    a = mxq(f64(kT), 1, "e4m3").transpose(0, 2, 1) @ mxq(f64(qT), 1, "e4m3")
    a = a + f64(kb)
    p = np.exp(a)
    w = p * f64(t)
    y = mxq(w, 1, "e4m3").transpose(0, 2, 1) @ mxq(f64(v), 1, "e4m3")
    y = y / (y[:, :, 127:128])
    return y

@@ -1,0 +1,197 @@
+from contextlib import ExitStack
+
+import concourse.mybir as mybir
+
+H, D, NQ, N = 4, 128, 512, 1024
+FLOPS = 2 * 2 * H * D * NQ * N
+
+F32 = mybir.dt.float32
+BF16 = mybir.dt.bfloat16
+U32 = mybir.dt.uint32
+U8 = mybir.dt.uint8
+FP8X4 = mybir.dt.float8_e4m3fn_x4
+ACT = mybir.ActivationFunctionType
+ALU = mybir.AluOpType
+
+P = 128
+PACK = 4
+ROWS = D // PACK
+PASS = P * PACK
+PASSES = N // PASS
+Q_SPLIT = 88
+LAST = H - 1
+LAST_BANKS = 3
+
+
+def tile_rows_kb_kernel(tc, qT, kT, t, v, kb, out):
+    nc = tc.nc
+    with ExitStack() as ctx:
+        sb = ctx.enter_context(tc.tile_pool(name="sb", bufs=1))
+        ps = ctx.enter_context(tc.psum_pool(name="ps", bufs=1))
+        ctx.enter_context(tc.manual_schedule())
+
+        def operand(name):
+            packed = sb.tile([P, PASS, PACK], BF16, name=name + "_bf", align_bytes=64)
+            codes = sb.tile([P, PASS], U32, name=name + "_codes", align_bytes=64)
+            scales = sb.tile([P, PASS], U8, name=name + "_scales", align_bytes=64)
+            return packed, codes, scales
+
+        def quantize(op, cols=slice(0, PASS)):
+            packed, codes, scales = op
+            nc.vector.quantize_mx(
+                out=codes[:, cols].bitcast(FP8X4),
+                scales=scales[:, cols],
+                in_=packed[:, cols, :].rearrange("p n j -> p (n j)"),
+            )
+
+        def product(acc, lhs, lhs_cols, rhs, rhs_cols, rows, start, stop):
+            nc.tensor.matmul_mx(
+                out=acc,
+                lhsT=lhs[1][rows, lhs_cols].bitcast(FP8X4),
+                lhsT_scale=lhs[2][rows, lhs_cols],
+                rhs=rhs[1][rows, rhs_cols].bitcast(FP8X4),
+                rhs_scale=rhs[2][rows, rhs_cols],
+                start=start,
+                stop=stop,
+            )
+
+        def block(i):
+            return slice(i * P, (i + 1) * P)
+
+        t_sb = sb.tile([P, PASSES, PACK], F32, name="t_sb")
+        kb_sb = sb.tile([P, PASSES, PACK], F32, name="kb_sb")
+        nc.scalar.dma_start(out=t_sb[:], in_=t.rearrange("(c p j) o -> p c (j o)", c=PASSES, j=PACK))
+        nc.scalar.dma_start(out=kb_sb[:], in_=kb.rearrange("(c p j) o -> p c (j o)", c=PASSES, j=PACK))
+
+        k_view = kT.rearrange("h (p j) n -> (h p) j n", j=PACK)
+        k_raw = [sb.tile([P, PACK, PASS], F32, name="k_raw%d" % c) for c in range(PASSES)]
+        v_raw = [sb.tile([P, H, PACK, D], F32, name="v_raw%d" % c) for c in range(PASSES)]
+        q_raw = sb.tile([P, PACK, NQ], F32, name="q_raw")
+        nc.sync.dma_start(out=k_raw[0][:], in_=k_view[:, :, 0:PASS])
+        nc.sync.dma_start(out=q_raw[:], in_=qT.rearrange("h (p j) n -> (h p) j n", j=PACK))
+        nc.sync.dma_start(out=k_raw[1][:], in_=k_view[:, :, PASS:N])
+        for c in range(PASSES):
+            nc.sync.dma_start(
+                out=v_raw[c][:].rearrange("p h j e -> p h (j e)"),
+                in_=v[:, c * PASS : (c + 1) * PASS, :].rearrange("h (p j) e -> p h (j e)", j=PACK),
+            )
+
+        q_op = operand("q")
+        k_op = [operand("k%d" % c) for c in range(PASSES)]
+        v_op = [operand("v%d" % c) for c in range(PASSES)]
+        w_op = [[operand("w%d_%d" % (h, c)) for c in range(PASSES)] for h in range(H)]
+        w_raw = [[sb.tile([P, PACK, NQ], BF16, name="w_raw%d_%d" % (h, c)) for c in range(PASSES)] for h in range(H)]
+
+        def small(name):
+            return sb.tile([P, PASSES, PACK], F32, name=name)
+
+        t_abs, t_step, t_sign = small("t_abs"), small("t_step"), small("t_sign")
+        log_t, inv_t, base, ratio, bias = small("log_t"), small("inv_t"), small("base"), small("ratio"), small("bias")
+
+        def flat(x):
+            return x[:].rearrange("p c j -> p (c j)")
+
+        nc.vector.scalar_tensor_tensor(out=flat(t_abs), in0=flat(t_sb), scalar=-1.0, in1=flat(t_sb), op0=ALU.mult, op1=ALU.max)
+        nc.vector.tensor_scalar(out=flat(t_step), in0=flat(t_sb), scalar1=0.0, scalar2=2.0, op0=ALU.is_ge, op1=ALU.mult)
+        nc.scalar.activation(out=flat(log_t), in_=flat(t_abs), func=ACT.Ln)
+        nc.scalar.activation(out=flat(inv_t), in_=flat(log_t), func=ACT.Exp, scale=-1.0)
+        nc.vector.tensor_scalar(out=flat(t_sign), in0=flat(t_step), scalar1=-1.0, scalar2=None, op0=ALU.add)
+        nc.vector.scalar_tensor_tensor(out=flat(base), in0=flat(log_t), scalar=-1.0, in1=flat(kb_sb), op0=ALU.add, op1=ALU.add)
+
+        def deal(copy, op, raw, cols):
+            copy(
+                out=op[0][:].rearrange("p (r s) j -> p s j r", r=PACK)[:, cols],
+                in_=raw[:].rearrange("p j (s r) -> p s j r", r=PACK)[:, cols],
+            )
+
+        deal(nc.vector.tensor_copy, k_op[0], k_raw[0], slice(0, P))
+        nc.vector.tensor_tensor(out=flat(ratio), in0=flat(t_abs), in1=flat(inv_t), op=ALU.mult)
+        quantize(k_op[0])
+        nc.vector.tensor_tensor(out=flat(bias), in0=flat(ratio), in1=flat(base), op=ALU.add)
+        deal(nc.vector.tensor_copy, q_op, q_raw, slice(0, Q_SPLIT))
+        deal(nc.scalar.copy, q_op, q_raw, slice(Q_SPLIT, P))
+        quantize(q_op)
+        deal(nc.vector.tensor_copy, k_op[1], k_raw[1], slice(0, P))
+        quantize(k_op[1])
+
+        def pack_values(c, h):
+            nc.vector.tensor_tensor(
+                out=v_op[c][0][:, block(h), :].rearrange("p (a i) j -> p a j i", i=4),
+                in0=v_raw[c][:, h].rearrange("p j (a i) -> p a j i", i=4),
+                in1=t_sign[:, c, :].unsqueeze(1).unsqueeze(3).to_broadcast([P, D // 4, PACK, 4]),
+                op=ALU.mult,
+            )
+
+        for h in range(H):
+            pack_values(0, h)
+        pack_values(1, 0)
+        quantize(v_op[0])
+        for h in range(1, H):
+            pack_values(1, h)
+
+        banks = [[ps.tile([P, NQ], F32, name="s%d_%d" % (h, b)) for b in range(LAST_BANKS if h == LAST else 1)] for h in range(H)]
+        steps = [(c, r) for c in range(PASSES) for r in range(PACK)]
+        slots = [(h, i) for i in range(len(steps)) for h in range(LAST)] + [(LAST, i) for i in range(len(steps))]
+        for h, i in slots:
+            c, r = steps[i]
+            bank = banks[h][i % len(banks[h])]
+            rows = slice(h * ROWS, (h + 1) * ROWS)
+            for m in range(NQ // P):
+                product(bank[:, block(m)], k_op[c], block(r), q_op, block(m), rows, True, True)
+            nc.scalar.activation(out=w_raw[h][c][:, r, :], in_=bank[:], func=ACT.Exp, bias=bias[:, c, r : r + 1])
+
+        sums = [ps.tile([P, PACK, D], F32, name="y%d" % b) for b in range(2)]
+
+        def span(tiles):
+            return slice(tiles.start * P, tiles.stop * P)
+
+        def pack_weights(h, c, tiles):
+            nc.vector.tensor_copy(
+                out=w_op[h][c][0][:, span(tiles), :].rearrange("p (a i) j -> p a j i", i=4),
+                in_=w_raw[h][c][:, :, span(tiles)].rearrange("p j (a i) -> p a j i", i=4),
+            )
+
+        def weighted_sums(h, tiles, acc):
+            for m in tiles:
+                for c in range(PASSES):
+                    product(acc[:, m, :], w_op[h][c], block(m), v_op[c], block(h), slice(0, P), c == 0, c == PASSES - 1)
+
+        def finish(h, tiles, acc):
+            ms = slice(tiles.start, tiles.stop)
+            inv = sb.tile([P, PACK, 1], F32, name="inv%d_%d" % (h, tiles.start))
+            res = sb.tile([P, PACK, D], F32, name="res%d_%d" % (h, tiles.start))
+            nc.vector.reciprocal(out=inv[:, ms, :], in_=acc[:, ms, D - 1 : D])
+            for m in tiles:
+                nc.scalar.activation(out=res[:, m, :], in_=acc[:, m, :], func=ACT.Copy, scale=inv[:, m, :])
+            nc.sync.dma_start(out=out[h].rearrange("(m t) e -> m t e", t=PACK)[:, ms, :], in_=res[:, ms, :])
+
+        whole, first, second = range(0, 4), range(0, 2), range(2, 4)
+        pack_weights(0, 0, whole)
+        quantize(v_op[1])
+        pack_weights(1, 0, whole)
+        quantize(w_op[0][0])
+        pack_weights(2, 0, whole)
+        quantize(w_op[1][0])
+        pack_weights(0, 1, whole)
+        quantize(w_op[2][0])
+        pack_weights(1, 1, whole)
+        quantize(w_op[0][1])
+        weighted_sums(0, whole, sums[0])
+        pack_weights(2, 1, whole)
+        quantize(w_op[1][1])
+        weighted_sums(1, whole, sums[1])
+        pack_weights(3, 0, whole)
+        quantize(w_op[2][1])
+        finish(0, whole, sums[0])
+        weighted_sums(2, whole, sums[0])
+        pack_weights(3, 1, first)
+        finish(1, whole, sums[1])
+        quantize(w_op[3][0])
+        pack_weights(3, 1, second)
+        quantize(w_op[3][1], span(first))
+        weighted_sums(3, first, sums[1])
+        finish(2, whole, sums[0])
+        quantize(w_op[3][1], span(second))
+        weighted_sums(3, second, sums[0])
+        finish(3, first, sums[1])
+        finish(3, second, sums[0])

@@ -19,8 +19,7 @@ ROWS = D // PACK
 PASS = P * PACK
 PASSES = N // PASS
 Q_SPLIT = 88
-LAST = H - 1
-LAST_BANKS = 3
+BANKS = (1, 1, 2, 2)
 
 
 def tile_rows_kb_kernel(tc, qT, kT, t, v, kb, out):
@@ -60,8 +59,8 @@ def tile_rows_kb_kernel(tc, qT, kT, t, v, kb, out):
 
         t_sb = sb.tile([P, PASSES, PACK], F32, name="t_sb")
         kb_sb = sb.tile([P, PASSES, PACK], F32, name="kb_sb")
-        nc.scalar.dma_start(out=t_sb[:], in_=t.rearrange("(c p j) o -> p c (j o)", c=PASSES, j=PACK))
-        nc.scalar.dma_start(out=kb_sb[:], in_=kb.rearrange("(c p j) o -> p c (j o)", c=PASSES, j=PACK))
+        nc.sync.dma_start(out=t_sb[:], in_=t.rearrange("(c p j) o -> p c (j o)", c=PASSES, j=PACK))
+        nc.sync.dma_start(out=kb_sb[:], in_=kb.rearrange("(c p j) o -> p c (j o)", c=PASSES, j=PACK))
 
         k_view = kT.rearrange("h (p j) n -> (h p) j n", j=PACK)
         k_raw = [sb.tile([P, PACK, PASS], F32, name="k_raw%d" % c) for c in range(PASSES)]
@@ -85,7 +84,8 @@ def tile_rows_kb_kernel(tc, qT, kT, t, v, kb, out):
         def small(name):
             return sb.tile([P, PASSES, PACK], F32, name=name)
 
-        t_abs, t_step, t_sign = small("t_abs"), small("t_step"), small("t_sign")
+        t_abs, t_step = small("t_abs"), small("t_step")
+        t_sign = sb.tile([P, PASSES, PACK], BF16, name="t_sign")
         log_t, inv_t, base, ratio, bias = small("log_t"), small("inv_t"), small("base"), small("ratio"), small("bias")
 
         def flat(x):
@@ -114,24 +114,30 @@ def tile_rows_kb_kernel(tc, qT, kT, t, v, kb, out):
         deal(nc.vector.tensor_copy, k_op[1], k_raw[1], slice(0, P))
         quantize(k_op[1])
 
-        def pack_values(c, h):
+        def pack_values(c):
+            nc.vector.tensor_copy(
+                out=v_op[c][0][:].rearrange("p (h a i) j -> p h a j i", h=H, i=4),
+                in_=v_raw[c][:].rearrange("p h j (a i) -> p h a j i", i=4),
+            )
+
+        def sign_values(c):
             nc.vector.tensor_tensor(
-                out=v_op[c][0][:, block(h), :].rearrange("p (a i) j -> p a j i", i=4),
-                in0=v_raw[c][:, h].rearrange("p j (a i) -> p a j i", i=4),
-                in1=t_sign[:, c, :].unsqueeze(1).unsqueeze(3).to_broadcast([P, D // 4, PACK, 4]),
+                out=v_op[c][0][:],
+                in0=v_op[c][0][:],
+                in1=t_sign[:, c, :].unsqueeze(1).to_broadcast([P, PASS, PACK]),
                 op=ALU.mult,
             )
 
-        for h in range(H):
-            pack_values(0, h)
-        pack_values(1, 0)
+        pack_values(0)
+        sign_values(0)
+        pack_values(1)
         quantize(v_op[0])
-        for h in range(1, H):
-            pack_values(1, h)
+        sign_values(1)
 
-        banks = [[ps.tile([P, NQ], F32, name="s%d_%d" % (h, b)) for b in range(LAST_BANKS if h == LAST else 1)] for h in range(H)]
+        banks = [[ps.tile([P, NQ], F32, name="s%d_%d" % (h, b)) for b in range(BANKS[h])] for h in range(H)]
         steps = [(c, r) for c in range(PASSES) for r in range(PACK)]
-        slots = [(h, i) for i in range(len(steps)) for h in range(LAST)] + [(LAST, i) for i in range(len(steps))]
+        slots = [slot for i in range(len(steps)) for slot in ((0, i), (1, i), (2 + i // PACK, i % PACK))]
+        slots = slots + [(h, i) for i in range(PACK, len(steps)) for h in (2, 3)]
         for h, i in slots:
             c, r = steps[i]
             bank = banks[h][i % len(banks[h])]
@@ -177,16 +183,16 @@ def tile_rows_kb_kernel(tc, qT, kT, t, v, kb, out):
         pack_weights(1, 1, whole)
         quantize(w_op[0][1])
         weighted_sums(0, whole, sums[0])
-        pack_weights(2, 1, whole)
+        pack_weights(3, 0, whole)
         quantize(w_op[1][1])
         weighted_sums(1, whole, sums[1])
-        pack_weights(3, 0, whole)
-        quantize(w_op[2][1])
-        finish(0, whole, sums[0])
-        weighted_sums(2, whole, sums[0])
-        pack_weights(3, 1, first)
-        finish(1, whole, sums[1])
         quantize(w_op[3][0])
+        pack_weights(2, 1, whole)
+        finish(0, whole, sums[0])
+        pack_weights(3, 1, first)
+        quantize(w_op[2][1])
+        weighted_sums(2, whole, sums[0])
+        finish(1, whole, sums[1])
         pack_weights(3, 1, second)
         quantize(w_op[3][1], span(first))
         weighted_sums(3, first, sums[1])

@@ -20,6 +20,8 @@ PASS = P * PACK
 PASSES = N // PASS
 Q_SPLIT = 88
 BANKS = (1, 1, 2, 2)
+WARM_FIRST = 12
+WARM_SLOT = 2
 
 
 def tile_rows_kb_kernel(tc, qT, kT, t, v, kb, out):
@@ -68,12 +70,16 @@ def tile_rows_kb_kernel(tc, qT, kT, t, v, kb, out):
         q_raw = sb.tile([P, PACK, NQ], F32, name="q_raw")
         nc.sync.dma_start(out=k_raw[0][:], in_=k_view[:, :, 0:PASS])
         nc.sync.dma_start(out=q_raw[:], in_=qT.rearrange("h (p j) n -> (h p) j n", j=PACK))
-        nc.sync.dma_start(out=k_raw[1][:], in_=k_view[:, :, PASS:N])
-        for c in range(PASSES):
+
+        def load_values(c):
             nc.sync.dma_start(
                 out=v_raw[c][:].rearrange("p h j e -> p h (j e)"),
                 in_=v[:, c * PASS : (c + 1) * PASS, :].rearrange("h (p j) e -> p h (j e)", j=PACK),
             )
+
+        load_values(0)
+        nc.sync.dma_start(out=k_raw[1][:], in_=k_view[:, :, PASS:N])
+        load_values(1)
 
         q_op = operand("q")
         k_op = [operand("k%d" % c) for c in range(PASSES)]
@@ -111,8 +117,6 @@ def tile_rows_kb_kernel(tc, qT, kT, t, v, kb, out):
         deal(nc.vector.tensor_copy, q_op, q_raw, slice(0, Q_SPLIT))
         deal(nc.scalar.copy, q_op, q_raw, slice(Q_SPLIT, P))
         quantize(q_op)
-        deal(nc.vector.tensor_copy, k_op[1], k_raw[1], slice(0, P))
-        quantize(k_op[1])
 
         def pack_values(c):
             nc.vector.tensor_copy(
@@ -130,11 +134,19 @@ def tile_rows_kb_kernel(tc, qT, kT, t, v, kb, out):
 
         pack_values(0)
         sign_values(0)
-        pack_values(1)
+        deal(nc.vector.tensor_copy, k_op[1], k_raw[1], slice(0, P))
         quantize(v_op[0])
-        sign_values(1)
+        quantize(k_op[1])
+        pack_values(1)
 
         banks = [[ps.tile([P, NQ], F32, name="s%d_%d" % (h, b)) for b in range(BANKS[h])] for h in range(H)]
+        sums = [ps.tile([P, PACK, D], F32, name="y%d" % b) for b in range(2)]
+
+        def keep_clock(count):
+            for n in range(count):
+                product(sums[0][:, n % PACK, :], k_op[0], block(0), k_op[0], block(1), slice(0, P), True, True)
+
+        keep_clock(WARM_FIRST)
         steps = [(c, r) for c in range(PASSES) for r in range(PACK)]
         slots = [slot for i in range(len(steps)) for slot in ((0, i), (1, i), (2 + i // PACK, i % PACK))]
         slots = slots + [(h, i) for i in range(PACK, len(steps)) for h in (2, 3)]
@@ -144,9 +156,9 @@ def tile_rows_kb_kernel(tc, qT, kT, t, v, kb, out):
             rows = slice(h * ROWS, (h + 1) * ROWS)
             for m in range(NQ // P):
                 product(bank[:, block(m)], k_op[c], block(r), q_op, block(m), rows, True, True)
+            keep_clock(WARM_SLOT)
             nc.scalar.activation(out=w_raw[h][c][:, r, :], in_=bank[:], func=ACT.Exp, bias=bias[:, c, r : r + 1])
 
-        sums = [ps.tile([P, PACK, D], F32, name="y%d" % b) for b in range(2)]
 
         def span(tiles):
             return slice(tiles.start * P, tiles.stop * P)
@@ -162,20 +174,21 @@ def tile_rows_kb_kernel(tc, qT, kT, t, v, kb, out):
                 for c in range(PASSES):
                     product(acc[:, m, :], w_op[h][c], block(m), v_op[c], block(h), slice(0, P), c == 0, c == PASSES - 1)
 
-        def finish(h, tiles, acc):
+        def finish(h, tiles, acc, queue=nc.sync):
             ms = slice(tiles.start, tiles.stop)
             inv = sb.tile([P, PACK, 1], F32, name="inv%d_%d" % (h, tiles.start))
             res = sb.tile([P, PACK, D], F32, name="res%d_%d" % (h, tiles.start))
             nc.vector.reciprocal(out=inv[:, ms, :], in_=acc[:, ms, D - 1 : D])
             for m in tiles:
                 nc.scalar.activation(out=res[:, m, :], in_=acc[:, m, :], func=ACT.Copy, scale=inv[:, m, :])
-            nc.sync.dma_start(out=out[h].rearrange("(m t) e -> m t e", t=PACK)[:, ms, :], in_=res[:, ms, :])
+            queue.dma_start(out=out[h].rearrange("(m t) e -> m t e", t=PACK)[:, ms, :], in_=res[:, ms, :])
 
         whole, first, second = range(0, 4), range(0, 2), range(2, 4)
         pack_weights(0, 0, whole)
-        quantize(v_op[1])
-        pack_weights(1, 0, whole)
+        sign_values(1)
         quantize(w_op[0][0])
+        pack_weights(1, 0, whole)
+        quantize(v_op[1])
         pack_weights(2, 0, whole)
         quantize(w_op[1][0])
         pack_weights(0, 1, whole)
@@ -200,4 +213,4 @@ def tile_rows_kb_kernel(tc, qT, kT, t, v, kb, out):
         quantize(w_op[3][1], span(second))
         weighted_sums(3, second, sums[0])
         finish(3, first, sums[1])
-        finish(3, second, sums[0])
+        finish(3, second, sums[0], nc.scalar)

@@ -20,8 +20,6 @@ PASS = P * PACK
 PASSES = N // PASS
 Q_SPLIT = 88
 BANKS = (1, 1, 2, 2)
-WARM_FIRST = 12
-WARM_SLOT = 2
 
 
 def tile_rows_kb_kernel(tc, qT, kT, t, v, kb, out):
@@ -77,8 +75,8 @@ def tile_rows_kb_kernel(tc, qT, kT, t, v, kb, out):
                 in_=v[:, c * PASS : (c + 1) * PASS, :].rearrange("h (p j) e -> p h (j e)", j=PACK),
             )
 
-        load_values(0)
         nc.sync.dma_start(out=k_raw[1][:], in_=k_view[:, :, PASS:N])
+        load_values(0)
         load_values(1)
 
         q_op = operand("q")
@@ -132,85 +130,95 @@ def tile_rows_kb_kernel(tc, qT, kT, t, v, kb, out):
                 op=ALU.mult,
             )
 
+        deal(nc.vector.tensor_copy, k_op[1], k_raw[1], slice(0, P))
+        quantize(k_op[1])
         pack_values(0)
         sign_values(0)
-        deal(nc.vector.tensor_copy, k_op[1], k_raw[1], slice(0, P))
-        quantize(v_op[0])
-        quantize(k_op[1])
         pack_values(1)
+        quantize(v_op[0])
+        sign_values(1)
 
         banks = [[ps.tile([P, NQ], F32, name="s%d_%d" % (h, b)) for b in range(BANKS[h])] for h in range(H)]
         sums = [ps.tile([P, PACK, D], F32, name="y%d" % b) for b in range(2)]
-
-        def keep_clock(count):
-            for n in range(count):
-                product(sums[0][:, n % PACK, :], k_op[0], block(0), k_op[0], block(1), slice(0, P), True, True)
-
-        keep_clock(WARM_FIRST)
         steps = [(c, r) for c in range(PASSES) for r in range(PACK)]
-        slots = [slot for i in range(len(steps)) for slot in ((0, i), (1, i), (2 + i // PACK, i % PACK))]
-        slots = slots + [(h, i) for i in range(PACK, len(steps)) for h in (2, 3)]
-        for h, i in slots:
+        slow = [(h, i) for i in range(len(steps)) for h in (0, 1)]
+        fast = [(h, i) for h in (2, 3) for i in range(len(steps))]
+        slots = [slot for pair in zip(slow, fast) for slot in pair]
+
+        def bank_of(slot):
+            h, i = slot
+            return banks[h][i % BANKS[h]]
+
+        def scores(slot, m):
+            h, i = slot
             c, r = steps[i]
-            bank = banks[h][i % len(banks[h])]
             rows = slice(h * ROWS, (h + 1) * ROWS)
-            for m in range(NQ // P):
-                product(bank[:, block(m)], k_op[c], block(r), q_op, block(m), rows, True, True)
-            keep_clock(WARM_SLOT)
-            nc.scalar.activation(out=w_raw[h][c][:, r, :], in_=bank[:], func=ACT.Exp, bias=bias[:, c, r : r + 1])
+            product(bank_of(slot)[:, block(m)], k_op[c], block(r), q_op, block(m), rows, True, True)
+
+        half = NQ // P // 2
+        for m in range(half):
+            scores(slots[0], m)
+        for n, slot in enumerate(slots):
+            for m in range(half):
+                scores(slot, half + m)
+                if n + 1 < len(slots):
+                    scores(slots[n + 1], m)
+            h, i = slot
+            c, r = steps[i]
+            nc.scalar.activation(out=w_raw[h][c][:, r, :], in_=bank_of(slot)[:], func=ACT.Exp, bias=bias[:, c, r : r + 1])
 
 
         def span(tiles):
             return slice(tiles.start * P, tiles.stop * P)
 
-        def pack_weights(h, c, tiles):
-            nc.vector.tensor_copy(
+        def pack_weights(copy, h, c, tiles):
+            copy(
                 out=w_op[h][c][0][:, span(tiles), :].rearrange("p (a i) j -> p a j i", i=4),
                 in_=w_raw[h][c][:, :, span(tiles)].rearrange("p j (a i) -> p a j i", i=4),
             )
 
-        def weighted_sums(h, tiles, acc):
-            for m in tiles:
+        whole, first, second = range(0, 4), range(0, 2), range(2, 4)
+
+        def weighted_sums(h, acc):
+            for m in whole:
                 for c in range(PASSES):
                     product(acc[:, m, :], w_op[h][c], block(m), v_op[c], block(h), slice(0, P), c == 0, c == PASSES - 1)
 
-        def finish(h, tiles, acc, queue=nc.sync):
-            ms = slice(tiles.start, tiles.stop)
-            inv = sb.tile([P, PACK, 1], F32, name="inv%d_%d" % (h, tiles.start))
-            res = sb.tile([P, PACK, D], F32, name="res%d_%d" % (h, tiles.start))
-            nc.vector.reciprocal(out=inv[:, ms, :], in_=acc[:, ms, D - 1 : D])
-            for m in tiles:
-                nc.scalar.activation(out=res[:, m, :], in_=acc[:, m, :], func=ACT.Copy, scale=inv[:, m, :])
-            queue.dma_start(out=out[h].rearrange("(m t) e -> m t e", t=PACK)[:, ms, :], in_=res[:, ms, :])
+        def finish(h, acc, on_vector):
+            inv = sb.tile([P, PACK, 1], F32, name="inv%d" % h)
+            res = sb.tile([P, PACK, D], F32, name="res%d" % h)
+            nc.vector.reciprocal(out=inv[:], in_=acc[:, :, D - 1 : D])
+            if on_vector:
+                nc.vector.tensor_tensor(out=res[:], in0=acc[:], in1=inv[:].to_broadcast([P, PACK, D]), op=ALU.mult)
+            else:
+                for m in whole:
+                    nc.scalar.activation(out=res[:, m, :], in_=acc[:, m, :], func=ACT.Copy, scale=inv[:, m, :])
+            nc.sync.dma_start(out=out[h].rearrange("(m t) e -> m t e", t=PACK), in_=res[:])
 
-        whole, first, second = range(0, 4), range(0, 2), range(2, 4)
-        pack_weights(0, 0, whole)
-        sign_values(1)
-        quantize(w_op[0][0])
-        pack_weights(1, 0, whole)
+        vector_copy = nc.vector.tensor_copy
+        pack_weights(vector_copy, 2, 0, whole)
         quantize(v_op[1])
-        pack_weights(2, 0, whole)
-        quantize(w_op[1][0])
-        pack_weights(0, 1, whole)
+        pack_weights(vector_copy, 0, 0, whole)
         quantize(w_op[2][0])
-        pack_weights(1, 1, whole)
-        quantize(w_op[0][1])
-        weighted_sums(0, whole, sums[0])
-        pack_weights(3, 0, whole)
-        quantize(w_op[1][1])
-        weighted_sums(1, whole, sums[1])
-        quantize(w_op[3][0])
-        pack_weights(2, 1, whole)
-        finish(0, whole, sums[0])
-        pack_weights(3, 1, first)
+        pack_weights(vector_copy, 1, 0, whole)
+        quantize(w_op[0][0])
+        pack_weights(vector_copy, 2, 1, whole)
+        quantize(w_op[1][0])
         quantize(w_op[2][1])
-        weighted_sums(2, whole, sums[0])
-        finish(1, whole, sums[1])
-        pack_weights(3, 1, second)
-        quantize(w_op[3][1], span(first))
-        weighted_sums(3, first, sums[1])
-        finish(2, whole, sums[0])
-        quantize(w_op[3][1], span(second))
-        weighted_sums(3, second, sums[0])
-        finish(3, first, sums[1])
-        finish(3, second, sums[0], nc.scalar)
+        weighted_sums(2, sums[0])
+        pack_weights(vector_copy, 3, 0, whole)
+        quantize(w_op[3][0])
+        pack_weights(vector_copy, 0, 1, whole)
+        quantize(w_op[0][1])
+        weighted_sums(0, sums[1])
+        pack_weights(nc.scalar.copy, 3, 1, second)
+        finish(2, sums[0], False)
+        pack_weights(vector_copy, 1, 1, whole)
+        finish(0, sums[1], False)
+        pack_weights(vector_copy, 3, 1, first)
+        quantize(w_op[1][1])
+        weighted_sums(1, sums[0])
+        quantize(w_op[3][1])
+        weighted_sums(3, sums[1])
+        finish(1, sums[0], False)
+        finish(3, sums[1], True)

@@ -18,7 +18,11 @@ PACK = 4
 ROWS = D // PACK
 PASS = P * PACK
 PASSES = N // PASS
-Q_SPLIT = 88
+HALF = NQ // 2
+EARLY = 8
+K_SPLIT = 88
+Q_SPLIT = 24
+W_SPLIT = 80
 BANKS = (1, 1, 2, 2)
 
 
@@ -29,13 +33,13 @@ def tile_rows_kb_kernel(tc, qT, kT, t, v, kb, out):
         ps = ctx.enter_context(tc.psum_pool(name="ps", bufs=1))
         ctx.enter_context(tc.manual_schedule())
 
-        def operand(name):
-            packed = sb.tile([P, PASS, PACK], BF16, name=name + "_bf", align_bytes=64)
-            codes = sb.tile([P, PASS], U32, name=name + "_codes", align_bytes=64)
-            scales = sb.tile([P, PASS], U8, name=name + "_scales", align_bytes=64)
+        def operand(name, width=PASS):
+            packed = sb.tile([P, width, PACK], BF16, name=name + "_bf", align_bytes=64)
+            codes = sb.tile([P, width], U32, name=name + "_codes", align_bytes=64)
+            scales = sb.tile([P, width], U8, name=name + "_scales", align_bytes=64)
             return packed, codes, scales
 
-        def quantize(op, cols=slice(0, PASS)):
+        def quantize(op, cols=slice(None)):
             packed, codes, scales = op
             nc.vector.quantize_mx(
                 out=codes[:, cols].bitcast(FP8X4),
@@ -60,30 +64,37 @@ def tile_rows_kb_kernel(tc, qT, kT, t, v, kb, out):
         t_sb = sb.tile([P, PASSES, PACK], F32, name="t_sb")
         kb_sb = sb.tile([P, PASSES, PACK], F32, name="kb_sb")
         nc.sync.dma_start(out=t_sb[:], in_=t.rearrange("(c p j) o -> p c (j o)", c=PASSES, j=PACK))
-        nc.sync.dma_start(out=kb_sb[:], in_=kb.rearrange("(c p j) o -> p c (j o)", c=PASSES, j=PACK))
 
         k_view = kT.rearrange("h (p j) n -> (h p) j n", j=PACK)
         k_raw = [sb.tile([P, PACK, PASS], F32, name="k_raw%d" % c) for c in range(PASSES)]
-        v_raw = [sb.tile([P, H, PACK, D], F32, name="v_raw%d" % c) for c in range(PASSES)]
-        q_raw = sb.tile([P, PACK, NQ], F32, name="q_raw")
+        v_raw = [[sb.tile([P, 2, PACK, D], F32, name="v_raw%d_%d" % (c, g)) for g in range(2)] for c in range(PASSES)]
+        q_raw = [sb.tile([P, PACK, HALF], F32, name="q_raw%d" % u) for u in range(2)]
+        q_view = qT.rearrange("h (p j) n -> (h p) j n", j=PACK)
         nc.sync.dma_start(out=k_raw[0][:], in_=k_view[:, :, 0:PASS])
-        nc.sync.dma_start(out=q_raw[:], in_=qT.rearrange("h (p j) n -> (h p) j n", j=PACK))
+        nc.sync.dma_start(out=kb_sb[:], in_=kb.rearrange("(c p j) o -> p c (j o)", c=PASSES, j=PACK))
 
-        def load_values(c):
+        def load_queries(u):
+            nc.sync.dma_start(out=q_raw[u][:], in_=q_view[:, :, u * HALF : (u + 1) * HALF])
+
+        def load_values(c, g):
             nc.sync.dma_start(
-                out=v_raw[c][:].rearrange("p h j e -> p h (j e)"),
-                in_=v[:, c * PASS : (c + 1) * PASS, :].rearrange("h (p j) e -> p h (j e)", j=PACK),
+                out=v_raw[c][g][:].rearrange("p h j e -> p h (j e)"),
+                in_=v[2 * g : 2 * g + 2, c * PASS : (c + 1) * PASS, :].rearrange("h (p j) e -> p h (j e)", j=PACK),
             )
 
+        load_queries(0)
+        load_values(0, 0)
+        load_queries(1)
+        load_values(0, 1)
         nc.sync.dma_start(out=k_raw[1][:], in_=k_view[:, :, PASS:N])
-        load_values(0)
-        load_values(1)
+        load_values(1, 0)
+        load_values(1, 1)
 
-        q_op = operand("q")
+        q_op = [operand("q%d" % u, HALF) for u in range(2)]
         k_op = [operand("k%d" % c) for c in range(PASSES)]
-        v_op = [operand("v%d" % c) for c in range(PASSES)]
+        v_op = [[operand("v%d_%d" % (c, g), 2 * D) for g in range(2)] for c in range(PASSES)]
         w_op = [[operand("w%d_%d" % (h, c)) for c in range(PASSES)] for h in range(H)]
-        w_raw = [[sb.tile([P, PACK, NQ], BF16, name="w_raw%d_%d" % (h, c)) for c in range(PASSES)] for h in range(H)]
+        w_raw = [[sb.tile([P, 2, PACK, HALF], BF16, name="w_raw%d_%d" % (h, c)) for c in range(PASSES)] for h in range(H)]
 
         def small(name):
             return sb.tile([P, PASSES, PACK], F32, name=name)
@@ -100,125 +111,181 @@ def tile_rows_kb_kernel(tc, qT, kT, t, v, kb, out):
         nc.scalar.activation(out=flat(log_t), in_=flat(t_abs), func=ACT.Ln)
         nc.scalar.activation(out=flat(inv_t), in_=flat(log_t), func=ACT.Exp, scale=-1.0)
         nc.vector.tensor_scalar(out=flat(t_sign), in0=flat(t_step), scalar1=-1.0, scalar2=None, op0=ALU.add)
-        nc.vector.scalar_tensor_tensor(out=flat(base), in0=flat(log_t), scalar=-1.0, in1=flat(kb_sb), op0=ALU.add, op1=ALU.add)
 
-        def deal(copy, op, raw, cols):
+        vector_copy, scalar_copy = nc.vector.tensor_copy, nc.scalar.copy
+
+        def deal_keys(copy, c, rows=slice(None)):
             copy(
-                out=op[0][:].rearrange("p (r s) j -> p s j r", r=PACK)[:, cols],
-                in_=raw[:].rearrange("p j (s r) -> p s j r", r=PACK)[:, cols],
+                out=k_op[c][0][:].rearrange("p (r s) j -> p s j r", r=PACK)[:, rows],
+                in_=k_raw[c][:].rearrange("p j (s r) -> p s j r", r=PACK)[:, rows],
             )
 
-        deal(nc.vector.tensor_copy, k_op[0], k_raw[0], slice(0, P))
-        nc.vector.tensor_tensor(out=flat(ratio), in0=flat(t_abs), in1=flat(inv_t), op=ALU.mult)
-        quantize(k_op[0])
-        nc.vector.tensor_tensor(out=flat(bias), in0=flat(ratio), in1=flat(base), op=ALU.add)
-        deal(nc.vector.tensor_copy, q_op, q_raw, slice(0, Q_SPLIT))
-        deal(nc.scalar.copy, q_op, q_raw, slice(Q_SPLIT, P))
-        quantize(q_op)
-
-        def pack_values(c):
-            nc.vector.tensor_copy(
-                out=v_op[c][0][:].rearrange("p (h a i) j -> p h a j i", h=H, i=4),
-                in_=v_raw[c][:].rearrange("p h j (a i) -> p h a j i", i=4),
+        def deal_queries(copy, u, quads=slice(None)):
+            copy(
+                out=q_op[u][0][:].rearrange("p (b a i) j -> p a j i b", b=2, i=2)[:, quads],
+                in_=q_raw[u][:].rearrange("p j (a i b) -> p a j i b", b=2, i=2)[:, quads],
             )
 
-        def sign_values(c):
+        def pack_values(c, g):
+            vector_copy(
+                out=v_op[c][g][0][:].rearrange("p (h a i) j -> p h a j i", h=2, i=4),
+                in_=v_raw[c][g][:].rearrange("p h j (a i) -> p h a j i", i=4),
+            )
+
+        def sign_values(c, g):
             nc.vector.tensor_tensor(
-                out=v_op[c][0][:],
-                in0=v_op[c][0][:],
-                in1=t_sign[:, c, :].unsqueeze(1).to_broadcast([P, PASS, PACK]),
+                out=v_op[c][g][0][:],
+                in0=v_op[c][g][0][:],
+                in1=t_sign[:, c, :].unsqueeze(1).to_broadcast([P, 2 * D, PACK]),
                 op=ALU.mult,
             )
 
-        deal(nc.vector.tensor_copy, k_op[1], k_raw[1], slice(0, P))
-        quantize(k_op[1])
-        pack_values(0)
-        sign_values(0)
-        pack_values(1)
-        quantize(v_op[0])
-        sign_values(1)
+        def pack_weights(copy, h, c, halves, cols=slice(None)):
+            copy(
+                out=w_op[h][c][0][:].rearrange("p (u n) j -> p u n j", u=2)[:, halves, cols, :].rearrange(
+                    "p u (a i) j -> p u a j i", i=4
+                ),
+                in_=w_raw[h][c][:, halves, :, cols].rearrange("p u j (a i) -> p u a j i", i=4),
+            )
 
-        banks = [[ps.tile([P, NQ], F32, name="s%d_%d" % (h, b)) for b in range(BANKS[h])] for h in range(H)]
+        banks = [[ps.tile([P, 2, HALF], F32, name="s%d_%d" % (h, b)) for b in range(BANKS[h])] for h in range(H)]
         sums = [ps.tile([P, PACK, D], F32, name="y%d" % b) for b in range(2)]
         steps = [(c, r) for c in range(PASSES) for r in range(PACK)]
         slow = [(h, i) for i in range(len(steps)) for h in (0, 1)]
-        fast = [(h, i) for h in (2, 3) for i in range(len(steps))]
+        fast = [(h, c * PACK + r) for c in range(PASSES) for h in (2, 3) for r in range(PACK)]
         slots = [slot for pair in zip(slow, fast) for slot in pair]
 
-        def bank_of(slot):
-            h, i = slot
-            return banks[h][i % BANKS[h]]
+        both, first, second = slice(0, 2), slice(0, 1), slice(1, 2)
+        pieces = [slot + (halves,) for halves in (first, second) for slot in slots[:EARLY]]
+        pieces = pieces + [slot + (both,) for slot in slots[EARLY:]]
 
-        def scores(slot, m):
-            h, i = slot
+        def columns(halves):
+            return slice(halves.start * HALF, halves.stop * HALF)
+
+        def score_calls(n):
+            if n == len(pieces):
+                return [], []
+            h, i, halves = pieces[n]
+            calls = [(h, i, u, b) for u in range(halves.start, halves.stop) for b in range(2)]
+            return calls[: len(calls) // 2], calls[len(calls) // 2 :]
+
+        def scores(h, i, u, b):
             c, r = steps[i]
             rows = slice(h * ROWS, (h + 1) * ROWS)
-            product(bank_of(slot)[:, block(m)], k_op[c], block(r), q_op, block(m), rows, True, True)
+            product(banks[h][i % BANKS[h]][:, u, block(b)], k_op[c], block(r), q_op[u], block(b), rows, True, True)
 
-        half = NQ // P // 2
-        for m in range(half):
-            scores(slots[0], m)
-        for n, slot in enumerate(slots):
-            for m in range(half):
-                scores(slot, half + m)
-                if n + 1 < len(slots):
-                    scores(slots[n + 1], m)
-            h, i = slot
-            c, r = steps[i]
-            nc.scalar.activation(out=w_raw[h][c][:, r, :], in_=bank_of(slot)[:], func=ACT.Exp, bias=bias[:, c, r : r + 1])
+        def weights(first_piece, last_piece):
+            for n in range(first_piece, last_piece):
+                late, early = score_calls(n)[1], score_calls(n + 1)[0]
+                for x in range(max(len(late), len(early))):
+                    for call in late[x : x + 1] + early[x : x + 1]:
+                        scores(*call)
+                h, i, halves = pieces[n]
+                c, r = steps[i]
+                nc.scalar.activation(
+                    out=w_raw[h][c][:, halves, r, :],
+                    in_=banks[h][i % BANKS[h]][:, halves, :],
+                    func=ACT.Exp,
+                    bias=bias[:, c, r : r + 1],
+                )
 
+        def weighted_sums(h, acc, halves):
+            for m in range(2 * halves.start, 2 * halves.stop):
+                for c in range(PASSES):
+                    product(acc[:, m, :], w_op[h][c], block(m), v_op[c][h // 2], block(h % 2), slice(0, P), c == 0, c == PASSES - 1)
 
-        def span(tiles):
-            return slice(tiles.start * P, tiles.stop * P)
+        inv = [sb.tile([P, PACK, 1], F32, name="inv%d" % h) for h in range(H)]
+        res = [sb.tile([P, PACK, D], F32, name="res%d" % h) for h in range(H)]
 
-        def pack_weights(copy, h, c, tiles):
-            copy(
-                out=w_op[h][c][0][:, span(tiles), :].rearrange("p (a i) j -> p a j i", i=4),
-                in_=w_raw[h][c][:, :, span(tiles)].rearrange("p j (a i) -> p a j i", i=4),
+        def invert(h, acc):
+            nc.vector.reciprocal(out=inv[h][:], in_=acc[:, :, D - 1 : D])
+
+        def store(h, halves):
+            nc.sync.dma_start(
+                out=out[h].rearrange("(u s b) e -> s u (b e)", u=2, b=2)[:, halves],
+                in_=res[h][:].rearrange("p (u b) e -> p u (b e)", u=2)[:, halves],
             )
 
-        whole, first, second = range(0, 4), range(0, 2), range(2, 4)
+        def divide_on_scalar(h, acc):
+            for m in range(PACK):
+                nc.scalar.activation(out=res[h][:, m, :], in_=acc[:, m, :], func=ACT.Copy, scale=inv[h][:, m, :])
+            store(h, both)
 
-        def weighted_sums(h, acc):
-            for m in whole:
-                for c in range(PASSES):
-                    product(acc[:, m, :], w_op[h][c], block(m), v_op[c], block(h), slice(0, P), c == 0, c == PASSES - 1)
+        def divide_on_vector(h, acc):
+            for halves in (first, second):
+                ms = slice(2 * halves.start, 2 * halves.stop)
+                nc.vector.tensor_tensor(
+                    out=res[h][:, ms, :], in0=acc[:, ms, :], in1=inv[h][:, ms, :].to_broadcast([P, 2, D]), op=ALU.mult
+                )
+                store(h, halves)
 
-        def finish(h, acc, on_vector):
-            inv = sb.tile([P, PACK, 1], F32, name="inv%d" % h)
-            res = sb.tile([P, PACK, D], F32, name="res%d" % h)
-            nc.vector.reciprocal(out=inv[:], in_=acc[:, :, D - 1 : D])
-            if on_vector:
-                nc.vector.tensor_tensor(out=res[:], in0=acc[:], in1=inv[:].to_broadcast([P, PACK, D]), op=ALU.mult)
-            else:
-                for m in whole:
-                    nc.scalar.activation(out=res[:, m, :], in_=acc[:, m, :], func=ACT.Copy, scale=inv[:, m, :])
-            nc.sync.dma_start(out=out[h].rearrange("(m t) e -> m t e", t=PACK), in_=res[:])
+        def finish_weights(h, acc, halves):
+            quantize(w_op[h][1], columns(halves))
+            weighted_sums(h, acc, halves)
 
-        vector_copy = nc.vector.tensor_copy
-        pack_weights(vector_copy, 2, 0, whole)
-        quantize(v_op[1])
-        pack_weights(vector_copy, 0, 0, whole)
-        quantize(w_op[2][0])
-        pack_weights(vector_copy, 1, 0, whole)
+        deal_keys(vector_copy, 0, slice(0, K_SPLIT))
+        deal_keys(scalar_copy, 0, slice(K_SPLIT, P))
+        nc.vector.scalar_tensor_tensor(out=flat(base), in0=flat(log_t), scalar=-1.0, in1=flat(kb_sb), op0=ALU.add, op1=ALU.add)
+        nc.vector.tensor_tensor(out=flat(ratio), in0=flat(t_abs), in1=flat(inv_t), op=ALU.mult)
+        quantize(k_op[0])
+        deal_queries(vector_copy, 0, slice(0, Q_SPLIT))
+        deal_queries(scalar_copy, 0, slice(Q_SPLIT, HALF // 4))
+        nc.vector.tensor_tensor(out=flat(bias), in0=flat(ratio), in1=flat(base), op=ALU.add)
+        quantize(q_op[0])
+        pack_values(0, 0)
+        sign_values(0, 0)
+        deal_queries(vector_copy, 1)
+        quantize(v_op[0][0])
+        quantize(q_op[1])
+        pack_values(0, 1)
+
+        for call in score_calls(0)[0]:
+            scores(*call)
+        weights(0, EARLY)
+
+        pack_weights(vector_copy, 2, 0, first)
+        sign_values(0, 1)
+        quantize(w_op[2][0], columns(first))
+        deal_keys(vector_copy, 1)
+        quantize(v_op[0][1])
+        quantize(k_op[1])
+        for g in range(2):
+            pack_values(1, g)
+        for g in range(2):
+            sign_values(1, g)
+        quantize(v_op[1][0])
+
+        weights(EARLY, len(pieces))
+
+        pack_weights(vector_copy, 2, 0, second)
+        quantize(v_op[1][1])
+        pack_weights(vector_copy, 0, 0, both)
+        quantize(w_op[2][0], columns(second))
+        pack_weights(vector_copy, 1, 0, both)
         quantize(w_op[0][0])
-        pack_weights(vector_copy, 2, 1, whole)
+        pack_weights(vector_copy, 3, 0, both)
         quantize(w_op[1][0])
-        quantize(w_op[2][1])
-        weighted_sums(2, sums[0])
-        pack_weights(vector_copy, 3, 0, whole)
+        pack_weights(vector_copy, 2, 1, both)
         quantize(w_op[3][0])
-        pack_weights(vector_copy, 0, 1, whole)
-        quantize(w_op[0][1])
-        weighted_sums(0, sums[1])
-        pack_weights(nc.scalar.copy, 3, 1, second)
-        finish(2, sums[0], False)
-        pack_weights(vector_copy, 1, 1, whole)
-        finish(0, sums[1], False)
-        pack_weights(vector_copy, 3, 1, first)
-        quantize(w_op[1][1])
-        weighted_sums(1, sums[0])
-        quantize(w_op[3][1])
-        weighted_sums(3, sums[1])
-        finish(1, sums[0], False)
-        finish(3, sums[1], True)
+        quantize(w_op[2][1])
+        weighted_sums(2, sums[0], both)
+        pack_weights(scalar_copy, 3, 1, both, slice(W_SPLIT, HALF))
+        pack_weights(vector_copy, 0, 1, first)
+        pack_weights(vector_copy, 0, 1, second)
+        finish_weights(0, sums[1], first)
+        finish_weights(0, sums[1], second)
+        invert(2, sums[0])
+        divide_on_scalar(2, sums[0])
+        pack_weights(vector_copy, 1, 1, first)
+        pack_weights(vector_copy, 1, 1, second)
+        finish_weights(1, sums[0], first)
+        invert(0, sums[1])
+        divide_on_scalar(0, sums[1])
+        pack_weights(vector_copy, 3, 1, both, slice(0, W_SPLIT))
+        finish_weights(1, sums[0], second)
+        finish_weights(3, sums[1], first)
+        finish_weights(3, sums[1], second)
+        invert(1, sums[0])
+        divide_on_scalar(1, sums[0])
+        invert(3, sums[1])
+        divide_on_vector(3, sums[1])

from contextlib import ExitStack

import concourse.mybir as mybir

H, D, NQ, N = 4, 128, 512, 1024
FLOPS = 2 * 2 * H * D * NQ * N

F32 = mybir.dt.float32
BF16 = mybir.dt.bfloat16
U32 = mybir.dt.uint32
U8 = mybir.dt.uint8
FP8X4 = mybir.dt.float8_e4m3fn_x4
ACT = mybir.ActivationFunctionType
ALU = mybir.AluOpType

P = 128
PACK = 4
ROWS = D // PACK
PASS = P * PACK
PASSES = N // PASS
HALF = NQ // 2
EARLY = 8
K_SPLIT = 88
Q_SPLIT = 24
W_SPLIT = 80
BANKS = (1, 1, 2, 2)


def tile_rows_kb_kernel(tc, qT, kT, t, v, kb, out):
    nc = tc.nc
    with ExitStack() as ctx:
        sb = ctx.enter_context(tc.tile_pool(name="sb", bufs=1))
        ps = ctx.enter_context(tc.psum_pool(name="ps", bufs=1))
        ctx.enter_context(tc.manual_schedule())

        def operand(name, width=PASS):
            packed = sb.tile([P, width, PACK], BF16, name=name + "_bf", align_bytes=64)
            codes = sb.tile([P, width], U32, name=name + "_codes", align_bytes=64)
            scales = sb.tile([P, width], U8, name=name + "_scales", align_bytes=64)
            return packed, codes, scales

        def quantize(op, cols=slice(None)):
            packed, codes, scales = op
            nc.vector.quantize_mx(
                out=codes[:, cols].bitcast(FP8X4),
                scales=scales[:, cols],
                in_=packed[:, cols, :].rearrange("p n j -> p (n j)"),
            )

        def product(acc, lhs, lhs_cols, rhs, rhs_cols, rows, start, stop):
            nc.tensor.matmul_mx(
                out=acc,
                lhsT=lhs[1][rows, lhs_cols].bitcast(FP8X4),
                lhsT_scale=lhs[2][rows, lhs_cols],
                rhs=rhs[1][rows, rhs_cols].bitcast(FP8X4),
                rhs_scale=rhs[2][rows, rhs_cols],
                start=start,
                stop=stop,
            )

        def block(i):
            return slice(i * P, (i + 1) * P)

        t_sb = sb.tile([P, PASSES, PACK], F32, name="t_sb")
        kb_sb = sb.tile([P, PASSES, PACK], F32, name="kb_sb")
        nc.sync.dma_start(out=t_sb[:], in_=t.rearrange("(c p j) o -> p c (j o)", c=PASSES, j=PACK))

        k_view = kT.rearrange("h (p j) n -> (h p) j n", j=PACK)
        k_raw = [sb.tile([P, PACK, PASS], F32, name="k_raw%d" % c) for c in range(PASSES)]
        v_raw = [[sb.tile([P, 2, PACK, D], F32, name="v_raw%d_%d" % (c, g)) for g in range(2)] for c in range(PASSES)]
        q_raw = [sb.tile([P, PACK, HALF], F32, name="q_raw%d" % u) for u in range(2)]
        q_view = qT.rearrange("h (p j) n -> (h p) j n", j=PACK)
        nc.sync.dma_start(out=k_raw[0][:], in_=k_view[:, :, 0:PASS])
        nc.sync.dma_start(out=kb_sb[:], in_=kb.rearrange("(c p j) o -> p c (j o)", c=PASSES, j=PACK))

        def load_queries(u):
            nc.sync.dma_start(out=q_raw[u][:], in_=q_view[:, :, u * HALF : (u + 1) * HALF])

        def load_values(c, g):
            nc.sync.dma_start(
                out=v_raw[c][g][:].rearrange("p h j e -> p h (j e)"),
                in_=v[2 * g : 2 * g + 2, c * PASS : (c + 1) * PASS, :].rearrange("h (p j) e -> p h (j e)", j=PACK),
            )

        load_queries(0)
        load_values(0, 0)
        load_queries(1)
        load_values(0, 1)
        nc.sync.dma_start(out=k_raw[1][:], in_=k_view[:, :, PASS:N])
        load_values(1, 0)
        load_values(1, 1)

        q_op = [operand("q%d" % u, HALF) for u in range(2)]
        k_op = [operand("k%d" % c) for c in range(PASSES)]
        v_op = [[operand("v%d_%d" % (c, g), 2 * D) for g in range(2)] for c in range(PASSES)]
        w_op = [[operand("w%d_%d" % (h, c)) for c in range(PASSES)] for h in range(H)]
        w_raw = [[sb.tile([P, 2, PACK, HALF], BF16, name="w_raw%d_%d" % (h, c)) for c in range(PASSES)] for h in range(H)]

        def small(name):
            return sb.tile([P, PASSES, PACK], F32, name=name)

        t_abs, t_step = small("t_abs"), small("t_step")
        t_sign = sb.tile([P, PASSES, PACK], BF16, name="t_sign")
        log_t, inv_t, base, ratio, bias = small("log_t"), small("inv_t"), small("base"), small("ratio"), small("bias")

        def flat(x):
            return x[:].rearrange("p c j -> p (c j)")

        nc.vector.scalar_tensor_tensor(out=flat(t_abs), in0=flat(t_sb), scalar=-1.0, in1=flat(t_sb), op0=ALU.mult, op1=ALU.max)
        nc.vector.tensor_scalar(out=flat(t_step), in0=flat(t_sb), scalar1=0.0, scalar2=2.0, op0=ALU.is_ge, op1=ALU.mult)
        nc.scalar.activation(out=flat(log_t), in_=flat(t_abs), func=ACT.Ln)
        nc.scalar.activation(out=flat(inv_t), in_=flat(log_t), func=ACT.Exp, scale=-1.0)
        nc.vector.tensor_scalar(out=flat(t_sign), in0=flat(t_step), scalar1=-1.0, scalar2=None, op0=ALU.add)

        vector_copy, scalar_copy = nc.vector.tensor_copy, nc.scalar.copy

        def deal_keys(copy, c, rows=slice(None)):
            copy(
                out=k_op[c][0][:].rearrange("p (r s) j -> p s j r", r=PACK)[:, rows],
                in_=k_raw[c][:].rearrange("p j (s r) -> p s j r", r=PACK)[:, rows],
            )

        def deal_queries(copy, u, quads=slice(None)):
            copy(
                out=q_op[u][0][:].rearrange("p (b a i) j -> p a j i b", b=2, i=2)[:, quads],
                in_=q_raw[u][:].rearrange("p j (a i b) -> p a j i b", b=2, i=2)[:, quads],
            )

        def pack_values(c, g):
            vector_copy(
                out=v_op[c][g][0][:].rearrange("p (h a i) j -> p h a j i", h=2, i=4),
                in_=v_raw[c][g][:].rearrange("p h j (a i) -> p h a j i", i=4),
            )

        def sign_values(c, g):
            nc.vector.tensor_tensor(
                out=v_op[c][g][0][:],
                in0=v_op[c][g][0][:],
                in1=t_sign[:, c, :].unsqueeze(1).to_broadcast([P, 2 * D, PACK]),
                op=ALU.mult,
            )

        def pack_weights(copy, h, c, halves, cols=slice(None)):
            copy(
                out=w_op[h][c][0][:].rearrange("p (u n) j -> p u n j", u=2)[:, halves, cols, :].rearrange(
                    "p u (a i) j -> p u a j i", i=4
                ),
                in_=w_raw[h][c][:, halves, :, cols].rearrange("p u j (a i) -> p u a j i", i=4),
            )

        banks = [[ps.tile([P, 2, HALF], F32, name="s%d_%d" % (h, b)) for b in range(BANKS[h])] for h in range(H)]
        sums = [ps.tile([P, PACK, D], F32, name="y%d" % b) for b in range(2)]
        steps = [(c, r) for c in range(PASSES) for r in range(PACK)]
        slow = [(h, i) for i in range(len(steps)) for h in (0, 1)]
        fast = [(h, c * PACK + r) for c in range(PASSES) for h in (2, 3) for r in range(PACK)]
        slots = [slot for pair in zip(slow, fast) for slot in pair]

        both, first, second = slice(0, 2), slice(0, 1), slice(1, 2)
        pieces = [slot + (halves,) for halves in (first, second) for slot in slots[:EARLY]]
        pieces = pieces + [slot + (both,) for slot in slots[EARLY:]]

        def columns(halves):
            return slice(halves.start * HALF, halves.stop * HALF)

        def score_calls(n):
            if n == len(pieces):
                return [], []
            h, i, halves = pieces[n]
            calls = [(h, i, u, b) for u in range(halves.start, halves.stop) for b in range(2)]
            return calls[: len(calls) // 2], calls[len(calls) // 2 :]

        def scores(h, i, u, b):
            c, r = steps[i]
            rows = slice(h * ROWS, (h + 1) * ROWS)
            product(banks[h][i % BANKS[h]][:, u, block(b)], k_op[c], block(r), q_op[u], block(b), rows, True, True)

        def weights(first_piece, last_piece):
            for n in range(first_piece, last_piece):
                late, early = score_calls(n)[1], score_calls(n + 1)[0]
                for x in range(max(len(late), len(early))):
                    for call in late[x : x + 1] + early[x : x + 1]:
                        scores(*call)
                h, i, halves = pieces[n]
                c, r = steps[i]
                nc.scalar.activation(
                    out=w_raw[h][c][:, halves, r, :],
                    in_=banks[h][i % BANKS[h]][:, halves, :],
                    func=ACT.Exp,
                    bias=bias[:, c, r : r + 1],
                )

        def weighted_sums(h, acc, halves):
            for m in range(2 * halves.start, 2 * halves.stop):
                for c in range(PASSES):
                    product(acc[:, m, :], w_op[h][c], block(m), v_op[c][h // 2], block(h % 2), slice(0, P), c == 0, c == PASSES - 1)

        inv = [sb.tile([P, PACK, 1], F32, name="inv%d" % h) for h in range(H)]
        res = [sb.tile([P, PACK, D], F32, name="res%d" % h) for h in range(H)]

        def invert(h, acc):
            nc.vector.reciprocal(out=inv[h][:], in_=acc[:, :, D - 1 : D])

        def store(h, halves):
            nc.sync.dma_start(
                out=out[h].rearrange("(u s b) e -> s u (b e)", u=2, b=2)[:, halves],
                in_=res[h][:].rearrange("p (u b) e -> p u (b e)", u=2)[:, halves],
            )

        def divide_on_scalar(h, acc):
            for m in range(PACK):
                nc.scalar.activation(out=res[h][:, m, :], in_=acc[:, m, :], func=ACT.Copy, scale=inv[h][:, m, :])
            store(h, both)

        def divide_on_vector(h, acc):
            for halves in (first, second):
                ms = slice(2 * halves.start, 2 * halves.stop)
                nc.vector.tensor_tensor(
                    out=res[h][:, ms, :], in0=acc[:, ms, :], in1=inv[h][:, ms, :].to_broadcast([P, 2, D]), op=ALU.mult
                )
                store(h, halves)

        def finish_weights(h, acc, halves):
            quantize(w_op[h][1], columns(halves))
            weighted_sums(h, acc, halves)

        deal_keys(vector_copy, 0, slice(0, K_SPLIT))
        deal_keys(scalar_copy, 0, slice(K_SPLIT, P))
        nc.vector.scalar_tensor_tensor(out=flat(base), in0=flat(log_t), scalar=-1.0, in1=flat(kb_sb), op0=ALU.add, op1=ALU.add)
        nc.vector.tensor_tensor(out=flat(ratio), in0=flat(t_abs), in1=flat(inv_t), op=ALU.mult)
        quantize(k_op[0])
        deal_queries(vector_copy, 0, slice(0, Q_SPLIT))
        deal_queries(scalar_copy, 0, slice(Q_SPLIT, HALF // 4))
        nc.vector.tensor_tensor(out=flat(bias), in0=flat(ratio), in1=flat(base), op=ALU.add)
        quantize(q_op[0])
        pack_values(0, 0)
        sign_values(0, 0)
        deal_queries(vector_copy, 1)
        quantize(v_op[0][0])
        quantize(q_op[1])
        pack_values(0, 1)

        for call in score_calls(0)[0]:
            scores(*call)
        weights(0, EARLY)

        pack_weights(vector_copy, 2, 0, first)
        sign_values(0, 1)
        quantize(w_op[2][0], columns(first))
        deal_keys(vector_copy, 1)
        quantize(v_op[0][1])
        quantize(k_op[1])
        for g in range(2):
            pack_values(1, g)
        for g in range(2):
            sign_values(1, g)
        quantize(v_op[1][0])

        weights(EARLY, len(pieces))

        pack_weights(vector_copy, 2, 0, second)
        quantize(v_op[1][1])
        pack_weights(vector_copy, 0, 0, both)
        quantize(w_op[2][0], columns(second))
        pack_weights(vector_copy, 1, 0, both)
        quantize(w_op[0][0])
        pack_weights(vector_copy, 3, 0, both)
        quantize(w_op[1][0])
        pack_weights(vector_copy, 2, 1, both)
        quantize(w_op[3][0])
        quantize(w_op[2][1])
        weighted_sums(2, sums[0], both)
        pack_weights(scalar_copy, 3, 1, both, slice(W_SPLIT, HALF))
        pack_weights(vector_copy, 0, 1, first)
        pack_weights(vector_copy, 0, 1, second)
        finish_weights(0, sums[1], first)
        finish_weights(0, sums[1], second)
        invert(2, sums[0])
        divide_on_scalar(2, sums[0])
        pack_weights(vector_copy, 1, 1, first)
        pack_weights(vector_copy, 1, 1, second)
        finish_weights(1, sums[0], first)
        invert(0, sums[1])
        divide_on_scalar(0, sums[1])
        pack_weights(vector_copy, 3, 1, both, slice(0, W_SPLIT))
        finish_weights(1, sums[0], second)
        finish_weights(3, sums[1], first)
        finish_weights(3, sums[1], second)
        invert(1, sums[0])
        divide_on_scalar(1, sums[0])
        invert(3, sums[1])
        divide_on_vector(3, sums[1])
